import numpy as np
import ml_dtypes


def mxq(x, axis, fmt="e4m3"):
    dtype, down = {"e4m3": (ml_dtypes.float8_e4m3fn, 7), "e5m2": (ml_dtypes.float8_e5m2, 14)}[fmt]
    v = np.moveaxis(np.asarray(x, np.float32).astype(ml_dtypes.bfloat16).astype(np.float64), axis, -1)
    blocks = v.reshape(v.shape[:-1] + (-1, 32))
    amax = np.abs(blocks).max(-1, keepdims=True)
    byte = np.maximum(np.where(amax > 0, np.frexp(amax)[1] - 1 + 127, 0) - down, 1)
    scale = np.exp2(byte - 127.0)
    codes = (blocks / scale).astype(np.float32).astype(dtype).astype(np.float64)
    return np.moveaxis((codes * scale).reshape(v.shape), -1, axis)


WIDE = False


def mx_kscale(k):
    if not WIDE:
        return np.ones(k)
    levels = np.array([10, -10, 5, -5, 0])
    if k % 512:
        return np.exp2(np.random.permutation(np.resize(levels, k // 32))).repeat(32)
    a = np.empty((k // 512, 16))
    for p in range(k // 512):
        a[p, :8] = np.random.permutation(np.resize(levels, 8))
        for g in range(8):
            far = levels[np.abs(levels - a[p, g]) >= 10]
            a[p, g + 8] = far[np.random.randint(len(far))]
    return np.exp2(a.ravel()).repeat(32)


BF16 = ml_dtypes.bfloat16


def bf(x):
    return np.asarray(x, np.float32).astype(BF16)


def f64(x):
    return np.asarray(x).astype(np.float64)

E4M3FN = np.array([(-1.0 if i & 128 else 1.0) * ((1.0 + (i & 7) / 8.0) * 2.0 ** (((i >> 3) & 15) - 7) if i & 120 else (i & 7) * 2.0 ** -9) for i in range(256)])


def e4m3fn_bytes(y):
    return np.clip(np.asarray(y, np.float64), -448.0, 448.0).astype(np.float32).astype(ml_dtypes.float8_e4m3fn).view(np.uint8)


def e4m3fn_values(b):
    return E4M3FN[b]


P, S, T = 4096, 512, 1024


def setup_inputs():
    s = mx_kscale(P)
    t = mx_kscale(S)
    strength = np.exp(0.5 * np.random.standard_normal((P, 1)))
    G = np.random.standard_normal((P, S)) * strength / np.sqrt(P) * s[:, None]
    G_scale = (np.max(np.abs(G), axis=1, keepdims=True) / 448).astype(np.float32)
    G_bytes = e4m3fn_bytes(G / np.repeat(f64(G_scale), S, axis=1))
    sigma = 0.4 + 0.4 * np.random.random_sample(S)
    E = np.random.standard_normal((S, T)) * sigma[:, None] * t[:, None]
    Q = np.linalg.qr(np.random.standard_normal((S, S)))[0]
    V = Q / sigma[None, :] / t[None, :]
    return {"G_bytes": G_bytes,
            "G_scale": G_scale,
            "J": bf(np.random.standard_normal((P, T)) / s[:, None]),
            "gain": bf((1 + 0.1 * np.random.standard_normal(S)) * t),
            "E": bf(E),
            "V": bf(V)}


def reference(G_bytes, G_scale, J, gain, E, V):
    G = e4m3fn_values(G_bytes) * np.repeat(f64(G_scale), S, axis=1)
    Gq = mxq(G, 0, "e4m3")
    Jq = mxq(f64(J), 0, "e4m3")
    F = Gq.T @ Jq
    B = F * f64(gain)[:, None] + f64(E)
    Y = mxq(f64(V), 1, "e4m3") @ mxq(B, 0, "e4m3")
    return Y

@@ -1,0 +1,281 @@
+from contextlib import ExitStack
+
+import concourse.mybir as mybir
+from concourse.masks import make_identity
+
+SRC, SEN, TIM = 4096, 512, 1024
+FLOPS = 2 * SRC * SEN * TIM + 2 * SEN * SEN * TIM
+
+F32 = mybir.dt.float32
+BF16 = mybir.dt.bfloat16
+U32 = mybir.dt.uint32
+U8 = mybir.dt.uint8
+FP8 = mybir.dt.float8_e4m3fn
+FP8X4 = mybir.dt.float8_e4m3fn_x4
+MULT = mybir.AluOpType.mult
+ADD = mybir.AluOpType.add
+COPY = mybir.ActivationFunctionType.Copy
+
+P = 128
+PASSES = SRC // 512
+NCH = 2
+W = TIM // NCH
+
+CFG = {'sj': ((1, 6, 7), (1, 2, 3, 4, 6)), 'vw': (3, 0, 1, 0, 0, 0, 0, 2), 'jfirst': 0, 'st': (3, 3, 4, 4), 'bi': (4, 1), 'bq': 5, 'ev': 7, 'vc': 6, 'vq': 5, 'tail': (1, 0), 'evv': (2, 5), 'lag': 0}
+
+
+def tile_meg_forward_whitened_d3_kernel(tc, g_bytes, g_scale, j_in, gain_in, e_in, v_in, out):
+    nc = tc.nc
+
+    with ExitStack() as ctx:
+        keep = ctx.enter_context(tc.tile_pool(name="keep", bufs=1))
+        work = ctx.enter_context(tc.tile_pool(name="work", bufs=3))
+        psum = ctx.enter_context(tc.psum_pool(name="psum", bufs=1))
+
+        ident = keep.tile([P, P], F32, name="ident")
+        make_identity(nc, ident[:])
+
+        gsc = keep.tile([P, PASSES, 4], F32, name="gsc")
+        gsc0 = keep.tile([P, 1, 4], F32, name="gsc0")
+        gs_view = g_scale.rearrange("(g p t) o -> p g (t o)", p=P, t=4)
+        gb_view = g_bytes.rearrange("(g p t) s -> g p t s", p=P, t=4)
+        j_view = j_in.rearrange("(g p t) n -> g p t n", p=P, t=4)
+        gb, jr = {}, {}
+
+        def load_g(g):
+            gb[g] = keep.tile([P, 4, SEN], U8, name="gb%d" % g, align_bytes=64)
+            nc.sync.dma_start(out=gb[g][:], in_=gb_view[g])
+
+        def load_j(c, g):
+            jr[c, g] = work.tile([P, 4, W], BF16, name="jr", bufs=12, align_bytes=64)
+            nc.sync.dma_start(out=jr[c, g][:], in_=j_view[g][:, :, c * W:(c + 1) * W])
+
+        nc.sync.dma_start(out=gsc0[:], in_=gs_view[:, 0:1, :])
+        load_g(0)
+        load_j(0, 0)
+        nc.sync.dma_start(out=gsc[:, 1:, :], in_=gs_view[:, 1:, :])
+        load_g(1)
+        load_j(0, 1)
+        v_raw = keep.tile([P, 4, SEN], BF16, name="v_raw", align_bytes=64)
+        for g in range(2, PASSES):
+            load_g(g)
+            load_j(0, g)
+            if g == 3:
+                nc.sync.dma_start(out=v_raw[:], in_=v_in.rearrange("(b p) s -> p b s", p=P))
+        gain = keep.tile([P, 4], BF16, name="gain")
+        nc.sync.dma_start(out=gain[:], in_=gain_in.rearrange("(p t) -> p t", t=4))
+        for g in range(PASSES):
+            load_j(1, g)
+            if g == 3:
+                e_sb = keep.tile([P, 4, TIM], BF16, name="e_sb", align_bytes=64)
+                nc.sync.dma_start(out=e_sb[:], in_=e_in.rearrange("(p t) n -> p t n", t=4))
+
+        gw, gi, ji = {}, {}, {}
+        gc, gs, jc, js = {}, {}, {}, {}
+        acc = {}
+        bank_of = {0: 0, 1: 4}
+
+        def widen(g, t, on_vector=False):
+            if t == 0:
+                gw[g] = work.tile([P, 4, SEN], BF16, name="gw", align_bytes=64)
+            sc = gsc0[:, 0, t:t + 1] if g == 0 else gsc[:, g, t:t + 1]
+            src = gb[g][:, t, :].bitcast(FP8)
+            if on_vector:
+                nc.vector.tensor_scalar(out=gw[g][:, t, :], in0=src, scalar1=sc, scalar2=None, op0=MULT)
+            else:
+                nc.scalar.activation(out=gw[g][:, t, :], in_=src, func=COPY, scale=sc)
+
+        def g_interleave(g):
+            gi[g] = work.tile([P, SEN, 4], BF16, name="gi", align_bytes=64)
+            nc.vector.tensor_copy(
+                out=gi[g][:].rearrange("p (t m) j -> p m j t", t=4),
+                in_=gw[g][:].rearrange("p j (m t) -> p m j t", t=4),
+            )
+
+        def g_quant(g):
+            gc[g] = keep.tile([P, SEN], U32, name="gc%d" % g, align_bytes=64)
+            gs[g] = keep.tile([P, SEN], U8, name="gs%d" % g, align_bytes=64)
+            nc.vector.quantize_mx(
+                out=gc[g][:].bitcast(FP8X4), scales=gs[g][:], in_=gi[g][:].rearrange("p n t -> p (n t)")
+            )
+
+        def j_interleave(c, g, on_scalar):
+            ji[c, g] = work.tile([P, W, 4], BF16, name="ji", bufs=6, align_bytes=64)
+            dst = ji[c, g][:].rearrange("p (c i) t -> p c t i", i=4)
+            src = jr[c, g][:].rearrange("p t (c i) -> p c t i", i=4)
+            if on_scalar:
+                nc.scalar.copy(out=dst, in_=src)
+            else:
+                nc.vector.tensor_copy(out=dst, in_=src)
+
+        def j_quant(c, g):
+            jc[c, g] = keep.tile([P, W], U32, name="jc%d_%d" % (c, g), align_bytes=64)
+            js[c, g] = keep.tile([P, W], U8, name="js%d_%d" % (c, g), align_bytes=64)
+            nc.vector.quantize_mx(
+                out=jc[c, g][:].bitcast(FP8X4), scales=js[c, g][:], in_=ji[c, g][:].rearrange("p n t -> p (n t)")
+            )
+
+        def stage1(c, g):
+            for m in range(4):
+                if g == 0:
+                    acc[c, m] = psum.tile([P, W], F32, name="bank%d" % (bank_of[c] + m))
+                nc.tensor.matmul_mx(
+                    out=acc[c, m][:],
+                    lhsT=gc[g][:, m * P:(m + 1) * P].bitcast(FP8X4),
+                    lhsT_scale=gs[g][:, m * P:(m + 1) * P],
+                    rhs=jc[c, g][:].bitcast(FP8X4),
+                    rhs_scale=js[c, g][:],
+                    start=(g == 0),
+                    stop=(g == PASSES - 1),
+                )
+
+        v_grp = keep.tile([P, SEN, 4], BF16, name="v_grp", align_bytes=64)
+        v_codes = keep.tile([P, SEN], U32, name="v_codes", align_bytes=64)
+        v_scales = keep.tile([P, SEN], U8, name="v_scales", align_bytes=64)
+        vt = {}
+
+        def v_transpose():
+            words = v_raw[:].rearrange("p b s -> p (b s)").bitcast(F32)
+            for h in range(2):
+                vt[h] = psum.tile([P, 2, 2, P], F32, name="bank%d" % (4 + h))
+                for b in range(2):
+                    for u in range(2):
+                        w0 = (2 * h + b) * 256
+                        nc.tensor.transpose(vt[h][:, b, u, :], words[:, w0 + u:w0 + 256:2], ident[:])
+
+        def v_copy(h):
+            dst = v_grp[:].rearrange("p w t -> p (w t)").bitcast(F32)[:, 512 * h:512 * (h + 1)]
+            nc.scalar.copy(
+                out=dst.rearrange("p (b r u) -> p b r u", b=2, u=2), in_=vt[h][:].rearrange("p b u r -> p b r u")
+            )
+
+        def v_quant():
+            nc.vector.quantize_mx(
+                out=v_codes[:].bitcast(FP8X4), scales=v_scales[:], in_=v_grp[:].rearrange("p w t -> p (w t)")
+            )
+
+        bp, bi, bc, bs, y, acc2 = {}, {}, {}, {}, {}, {}
+
+        def gain_noise(c, m, h, parts):
+            n = W // parts
+            if m == 0:
+                bp[c, h] = work.tile([P, 4, n], BF16, name="bp%d" % n, bufs=parts, align_bytes=64)
+            nc.vector.scalar_tensor_tensor(
+                out=bp[c, h][:, m, :],
+                in0=acc[c, m][:, h * n:(h + 1) * n],
+                scalar=gain[:, m:m + 1],
+                in1=e_sb[:, m, c * W + h * n:c * W + (h + 1) * n],
+                op0=MULT,
+                op1=ADD,
+            )
+
+        def b_interleave(c, h, parts, on_scalar):
+            n = W // parts
+            bi[c, h] = work.tile([P, n, 4], BF16, name="bi%d" % n, bufs=parts, align_bytes=64)
+            dst = bi[c, h][:].rearrange("p (c i) t -> p c t i", i=4)
+            src = bp[c, h][:].rearrange("p t (c i) -> p c t i", i=4)
+            if on_scalar:
+                nc.scalar.copy(out=dst, in_=src)
+            else:
+                nc.vector.tensor_copy(out=dst, in_=src)
+
+        def b_quant(c, h, parts):
+            n = W // parts
+            bc[c, h] = work.tile([P, n], U32, name="bc%d" % n, bufs=parts, align_bytes=64)
+            bs[c, h] = work.tile([P, n], U8, name="bs%d" % n, bufs=parts, align_bytes=64)
+            nc.vector.quantize_mx(
+                out=bc[c, h][:].bitcast(FP8X4), scales=bs[c, h][:], in_=bi[c, h][:].rearrange("p n t -> p (n t)")
+            )
+
+        def stage2(c, h, parts):
+            n = W // parts
+            for b in range(4):
+                bank = (0 if c == 0 else 4 * h) + b
+                acc2[c, h, b] = psum.tile([P, n], F32, name="bank%d" % bank)
+                nc.tensor.matmul_mx(
+                    out=acc2[c, h, b][:],
+                    lhsT=v_codes[:, b * P:(b + 1) * P].bitcast(FP8X4),
+                    lhsT_scale=v_scales[:, b * P:(b + 1) * P],
+                    rhs=bc[c, h][:].bitcast(FP8X4),
+                    rhs_scale=bs[c, h][:],
+                    start=True,
+                    stop=True,
+                )
+
+        def finish(c, h, b, parts, on_scalar):
+            n = W // parts
+            y = work.tile([P, n], F32, name="y%d" % n, bufs=4)
+            if on_scalar:
+                nc.scalar.copy(out=y[:], in_=acc2[c, h, b][:])
+            else:
+                nc.vector.tensor_copy(out=y[:], in_=acc2[c, h, b][:])
+            nc.sync.dma_start(out=out[b * P:(b + 1) * P, c * W + h * n:c * W + (h + 1) * n], in_=y[:])
+
+        with tc.manual_schedule():
+            pending = []
+
+            def flush(keep_back):
+                while len(pending) > keep_back:
+                    c, g = pending.pop(0)
+                    j_quant(c, g)
+                    stage1(c, g)
+
+            def widen_all(g):
+                for t in range(4):
+                    widen(g, t, on_vector=t >= 4 - CFG["vw"][g])
+
+            widen_all(0)
+            for g in range(PASSES):
+                on_scalar = g in CFG["sj"][0]
+                if on_scalar and CFG["jfirst"]:
+                    j_interleave(0, g, True)
+                if g + 1 < PASSES:
+                    widen_all(g + 1)
+                if on_scalar and not CFG["jfirst"]:
+                    j_interleave(0, g, True)
+                if g == 3:
+                    v_transpose()
+                if g == CFG["vc"]:
+                    v_copy(0)
+                    v_copy(1)
+                g_interleave(g)
+                if not on_scalar:
+                    j_interleave(0, g, False)
+                flush(CFG["lag"])
+                g_quant(g)
+                pending.append((0, g))
+                if not on_scalar:
+                    flush(CFG["lag"])
+            for g in range(PASSES):
+                on_scalar = g in CFG["sj"][1]
+                j_interleave(1, g, on_scalar)
+                flush(0 if g == 0 else CFG["lag"])
+                if g == CFG["vq"]:
+                    v_quant()
+                for m in range(4):
+                    if CFG["st"][m] == g:
+                        gain_noise(0, m, 0, 1)
+                pending.append((1, g))
+                if not on_scalar:
+                    flush(CFG["lag"])
+                if g == CFG["bi"][0]:
+                    b_interleave(0, 0, 1, CFG["bi"][1])
+                if g == CFG["bq"]:
+                    b_quant(0, 0, 1)
+                    stage2(0, 0, 1)
+                if g == CFG["ev"]:
+                    for b in range(4):
+                        finish(0, 0, b, 1, True)
+            flush(0)
+            for h in range(2):
+                for m in range(4):
+                    gain_noise(1, m, h, 2)
+                if h == 1:
+                    b_quant(1, 0, 2)
+                    stage2(1, 0, 2)
+                b_interleave(1, h, 2, CFG["tail"][h])
+            b_quant(1, 1, 2)
+            stage2(1, 1, 2)
+            for h in range(2):
+                for b in range(4):
+                    finish(1, h, b, 2, (4 * h + b) not in CFG["evv"])

@@ -21,7 +21,7 @@ PASSES = SRC // 512
 NCH = 2
 W = TIM // NCH
 
-CFG = {'sj': ((1, 6, 7), (1, 2, 3, 4, 6)), 'vw': (3, 0, 1, 0, 0, 0, 0, 2), 'jfirst': 0, 'st': (3, 3, 4, 4), 'bi': (4, 1), 'bq': 5, 'ev': 7, 'vc': 6, 'vq': 5, 'tail': (1, 0), 'evv': (2, 5), 'lag': 0}
+CFG = {'sj': ((3, 4, 7), (0, 2, 4, 5, 6)), 'vw': (3, 0, 0, 0, 0, 1, 0, 0), 'jfirst': 0, 'st': (1, 1, 3, 4), 'bi': (7, 1), 'bq': 7, 'ev': 7, 'vc': 5, 'vq': 7, 'tail': (0, 0), 'evv': (2, 3, 4, 5), 'lag': 0, 'pj': ((), ()), 'late': 0, 'gfirst': 1, 'form': 0}
 
 
 def tile_meg_forward_whitened_d3_kernel(tc, g_bytes, g_scale, j_in, gain_in, e_in, v_in, out):
@@ -34,6 +34,8 @@ def tile_meg_forward_whitened_d3_kernel(tc, g_bytes, g_scale, j_in, gain_in, e_i
 
         ident = keep.tile([P, P], F32, name="ident")
         make_identity(nc, ident[:])
+        ident_b = keep.tile([P, P], BF16, name="ident_b")
+        make_identity(nc, ident_b[:])
 
         gsc = keep.tile([P, PASSES, 4], F32, name="gsc")
         gsc0 = keep.tile([P, 1, 4], F32, name="gsc0")
@@ -50,15 +52,14 @@ def tile_meg_forward_whitened_d3_kernel(tc, g_bytes, g_scale, j_in, gain_in, e_i
             jr[c, g] = work.tile([P, 4, W], BF16, name="jr", bufs=12, align_bytes=64)
             nc.sync.dma_start(out=jr[c, g][:], in_=j_view[g][:, :, c * W:(c + 1) * W])
 
-        nc.sync.dma_start(out=gsc0[:], in_=gs_view[:, 0:1, :])
-        load_g(0)
-        load_j(0, 0)
-        nc.sync.dma_start(out=gsc[:, 1:, :], in_=gs_view[:, 1:, :])
-        load_g(1)
-        load_j(0, 1)
+        nc.scalar.dma_start(out=gsc0[:], in_=gs_view[:, 0:1, :])
+        nc.scalar.dma_start(out=gsc[:, 1:, :], in_=gs_view[:, 1:, :])
         v_raw = keep.tile([P, 4, SEN], BF16, name="v_raw", align_bytes=64)
-        for g in range(2, PASSES):
+        for g in range(CFG["gfirst"]):
             load_g(g)
+        for g in range(PASSES):
+            if g + CFG["gfirst"] < PASSES:
+                load_g(g + CFG["gfirst"])
             load_j(0, g)
             if g == 3:
                 nc.sync.dma_start(out=v_raw[:], in_=v_in.rearrange("(b p) s -> p b s", p=P))
@@ -73,7 +74,8 @@ def tile_meg_forward_whitened_d3_kernel(tc, g_bytes, g_scale, j_in, gain_in, e_i
         gw, gi, ji = {}, {}, {}
         gc, gs, jc, js = {}, {}, {}, {}
         acc = {}
-        bank_of = {0: 0, 1: 4}
+        bank_of = {0: 0, 1: 0 if CFG["late"] else 4}
+        turn = [0]
 
         def widen(g, t, on_vector=False):
             if t == 0:
@@ -107,6 +109,32 @@ def tile_meg_forward_whitened_d3_kernel(tc, g_bytes, g_scale, j_in, gain_in, e_i
                 nc.scalar.copy(out=dst, in_=src)
             else:
                 nc.vector.tensor_copy(out=dst, in_=src)
+
+        def j_interleave_pe(c, g):
+            ji[c, g] = work.tile([P, W, 4], BF16, name="ji", bufs=6, align_bytes=64)
+            flat = ji[c, g][:].rearrange("p n t -> p (n t)")
+            for q in range(2):
+                xp = psum.tile([P, 1024], BF16, name="bank%d" % (4 + turn[0] % 4))
+                turn[0] += 1
+                for h in range(2):
+                    n0 = 256 * q + 128 * h
+                    if CFG["form"] == 0:
+                        nc.tensor.matmul(
+                            out=xp[:, 512 * h:512 * (h + 1)].rearrange("p (n t) -> p t n", t=4),
+                            lhsT=ident_b[:],
+                            rhs=jr[c, g][:, :, n0:n0 + 128],
+                            start=True,
+                            stop=True,
+                        )
+                    else:
+                        nc.tensor.matmul(
+                            out=xp[:, 512 * h:512 * (h + 1)].rearrange("p (n t) -> p n t", t=4),
+                            lhsT=ident_b[:],
+                            rhs=jr[c, g][:, :, n0:n0 + 128].rearrange("p t n -> p n t"),
+                            start=True,
+                            stop=True,
+                        )
+                nc.scalar.copy(out=flat[:, 1024 * q:1024 * (q + 1)], in_=xp[:])
 
         def j_quant(c, g):
             jc[c, g] = keep.tile([P, W], U32, name="jc%d_%d" % (c, g), align_bytes=64)
@@ -190,7 +218,9 @@ def tile_meg_forward_whitened_d3_kernel(tc, g_bytes, g_scale, j_in, gain_in, e_i
         def stage2(c, h, parts):
             n = W // parts
             for b in range(4):
-                bank = (0 if c == 0 else 4 * h) + b
+                bank = ((4 if CFG["late"] else 0) if c == 0 else 4 * h) + b
+                if c == 1 and CFG["late"]:
+                    bank = 4 * (1 - h) + b
                 acc2[c, h, b] = psum.tile([P, n], F32, name="bank%d" % bank)
                 nc.tensor.matmul_mx(
                     out=acc2[c, h, b][:],
@@ -204,7 +234,7 @@ def tile_meg_forward_whitened_d3_kernel(tc, g_bytes, g_scale, j_in, gain_in, e_i
 
         def finish(c, h, b, parts, on_scalar):
             n = W // parts
-            y = work.tile([P, n], F32, name="y%d" % n, bufs=4)
+            y = work.tile([P, n], F32, name="y%d" % n, bufs=4 * parts)
             if on_scalar:
                 nc.scalar.copy(out=y[:], in_=acc2[c, h, b][:])
             else:
@@ -214,11 +244,16 @@ def tile_meg_forward_whitened_d3_kernel(tc, g_bytes, g_scale, j_in, gain_in, e_i
         with tc.manual_schedule():
             pending = []
 
+            held = []
+
             def flush(keep_back):
                 while len(pending) > keep_back:
                     c, g = pending.pop(0)
                     j_quant(c, g)
-                    stage1(c, g)
+                    if CFG["late"] and c == 1 and not bp.get("done"):
+                        held.append(g)
+                    else:
+                        stage1(c, g)
 
             def widen_all(g):
                 for t in range(4):
@@ -227,15 +262,16 @@ def tile_meg_forward_whitened_d3_kernel(tc, g_bytes, g_scale, j_in, gain_in, e_i
             widen_all(0)
             for g in range(PASSES):
                 on_scalar = g in CFG["sj"][0]
+                on_scalar = on_scalar or g in CFG["pj"][0]
+                do_s = j_interleave_pe if g in CFG["pj"][0] else (lambda c, g: j_interleave(c, g, True))
                 if on_scalar and CFG["jfirst"]:
-                    j_interleave(0, g, True)
+                    do_s(0, g)
                 if g + 1 < PASSES:
                     widen_all(g + 1)
                 if on_scalar and not CFG["jfirst"]:
-                    j_interleave(0, g, True)
-                if g == 3:
-                    v_transpose()
+                    do_s(0, g)
                 if g == CFG["vc"]:
+                    v_transpose()
                     v_copy(0)
                     v_copy(1)
                 g_interleave(g)
@@ -248,13 +284,22 @@ def tile_meg_forward_whitened_d3_kernel(tc, g_bytes, g_scale, j_in, gain_in, e_i
                     flush(CFG["lag"])
             for g in range(PASSES):
                 on_scalar = g in CFG["sj"][1]
-                j_interleave(1, g, on_scalar)
+                on_scalar = on_scalar or g in CFG["pj"][1]
+                if g in CFG["pj"][1]:
+                    j_interleave_pe(1, g)
+                else:
+                    j_interleave(1, g, on_scalar)
                 flush(0 if g == 0 else CFG["lag"])
                 if g == CFG["vq"]:
                     v_quant()
                 for m in range(4):
                     if CFG["st"][m] == g:
                         gain_noise(0, m, 0, 1)
+                        if m == 3:
+                            bp["done"] = True
+                            for k in held:
+                                stage1(1, k)
+                            held.clear()
                 pending.append((1, g))
                 if not on_scalar:
                     flush(CFG["lag"])

@@ -21,7 +21,7 @@ PASSES = SRC // 512
 NCH = 2
 W = TIM // NCH
 
-CFG = {'sj': ((3, 4, 7), (0, 2, 4, 5, 6)), 'vw': (3, 0, 0, 0, 0, 1, 0, 0), 'jfirst': 0, 'st': (1, 1, 3, 4), 'bi': (7, 1), 'bq': 7, 'ev': 7, 'vc': 5, 'vq': 7, 'tail': (0, 0), 'evv': (2, 3, 4, 5), 'lag': 0, 'pj': ((), ()), 'late': 0, 'gfirst': 1, 'form': 0}
+CFG = {'sj': ((0, 4, 5, 6, 7), (2, 3, 5, 6)), 'vw': (3, 1, 0, 0, 0, 0, 0, 0), 'jfirst': 0, 'st': (1, 1, 1, 5), 'bi': (6, 1), 'bq': 7, 'ev': 7, 'vc': 7, 'vq': 7, 'tail': (0, 0), 'evv': (4,), 'lag': 0, 'pj': ((0, 5, 6, 7), ()), 'late': 0, 'gfirst': 1, 'form': 1}
 
 
 def tile_meg_forward_whitened_d3_kernel(tc, g_bytes, g_scale, j_in, gain_in, e_in, v_in, out):
@@ -46,7 +46,10 @@ def tile_meg_forward_whitened_d3_kernel(tc, g_bytes, g_scale, j_in, gain_in, e_i
 
         def load_g(g):
             gb[g] = keep.tile([P, 4, SEN], U8, name="gb%d" % g, align_bytes=64)
-            nc.sync.dma_start(out=gb[g][:], in_=gb_view[g])
+            for t in range(0, 4, 2) if g == 0 else ():
+                nc.sync.dma_start(out=gb[g][:, t:t + 2, :], in_=gb_view[g][:, t:t + 2, :])
+            if g > 0:
+                nc.sync.dma_start(out=gb[g][:], in_=gb_view[g])
 
         def load_j(c, g):
             jr[c, g] = work.tile([P, 4, W], BF16, name="jr", bufs=12, align_bytes=64)

@@ -21,7 +21,7 @@ PASSES = SRC // 512
 NCH = 2
 W = TIM // NCH
 
-CFG = {'sj': ((0, 4, 5, 6, 7), (2, 3, 5, 6)), 'vw': (3, 1, 0, 0, 0, 0, 0, 0), 'jfirst': 0, 'st': (1, 1, 1, 5), 'bi': (6, 1), 'bq': 7, 'ev': 7, 'vc': 7, 'vq': 7, 'tail': (0, 0), 'evv': (4,), 'lag': 0, 'pj': ((0, 5, 6, 7), ()), 'late': 0, 'gfirst': 1, 'form': 1}
+CFG = {'sj': ((3, 4, 7), (0, 2, 4, 5, 6)), 'vw': (3, 0, 0, 0, 0, 1, 0, 0), 'jfirst': 0, 'st': (1, 1, 3, 4), 'bi': (7, 1), 'bq': 7, 'ev': 7, 'vc': 5, 'vq': 7, 'tail': (0, 0), 'evv': (2, 3, 4, 5), 'lag': 0, 'pj': ((), ()), 'late': 0, 'gfirst': 1, 'form': 0}
 
 
 def tile_meg_forward_whitened_d3_kernel(tc, g_bytes, g_scale, j_in, gain_in, e_in, v_in, out):
@@ -32,13 +32,12 @@ def tile_meg_forward_whitened_d3_kernel(tc, g_bytes, g_scale, j_in, gain_in, e_i
         work = ctx.enter_context(tc.tile_pool(name="work", bufs=3))
         psum = ctx.enter_context(tc.psum_pool(name="psum", bufs=1))
 
+        ident_raw = keep.tile([P, P], F32, name="ident_raw")
+        make_identity(nc, ident_raw[:])
         ident = keep.tile([P, P], F32, name="ident")
-        make_identity(nc, ident[:])
-        ident_b = keep.tile([P, P], BF16, name="ident_b")
-        make_identity(nc, ident_b[:])
+        nc.scalar.activation(out=ident[:], in_=ident_raw[:], func=COPY)
 
-        gsc = keep.tile([P, PASSES, 4], F32, name="gsc")
-        gsc0 = keep.tile([P, 1, 4], F32, name="gsc0")
+        gsc = {}
         gs_view = g_scale.rearrange("(g p t) o -> p g (t o)", p=P, t=4)
         gb_view = g_bytes.rearrange("(g p t) s -> g p t s", p=P, t=4)
         j_view = j_in.rearrange("(g p t) n -> g p t n", p=P, t=4)
@@ -46,6 +45,8 @@ def tile_meg_forward_whitened_d3_kernel(tc, g_bytes, g_scale, j_in, gain_in, e_i
 
         def load_g(g):
             gb[g] = keep.tile([P, 4, SEN], U8, name="gb%d" % g, align_bytes=64)
+            gsc[g] = keep.tile([P, 1, 4], F32, name="gsc%d" % g)
+            nc.sync.dma_start(out=gsc[g][:], in_=gs_view[:, g:g + 1, :])
             for t in range(0, 4, 2) if g == 0 else ():
                 nc.sync.dma_start(out=gb[g][:, t:t + 2, :], in_=gb_view[g][:, t:t + 2, :])
             if g > 0:
@@ -55,8 +56,6 @@ def tile_meg_forward_whitened_d3_kernel(tc, g_bytes, g_scale, j_in, gain_in, e_i
             jr[c, g] = work.tile([P, 4, W], BF16, name="jr", bufs=12, align_bytes=64)
             nc.sync.dma_start(out=jr[c, g][:], in_=j_view[g][:, :, c * W:(c + 1) * W])
 
-        nc.scalar.dma_start(out=gsc0[:], in_=gs_view[:, 0:1, :])
-        nc.scalar.dma_start(out=gsc[:, 1:, :], in_=gs_view[:, 1:, :])
         v_raw = keep.tile([P, 4, SEN], BF16, name="v_raw", align_bytes=64)
         for g in range(CFG["gfirst"]):
             load_g(g)
@@ -83,7 +82,7 @@ def tile_meg_forward_whitened_d3_kernel(tc, g_bytes, g_scale, j_in, gain_in, e_i
         def widen(g, t, on_vector=False):
             if t == 0:
                 gw[g] = work.tile([P, 4, SEN], BF16, name="gw", align_bytes=64)
-            sc = gsc0[:, 0, t:t + 1] if g == 0 else gsc[:, g, t:t + 1]
+            sc = gsc[g][:, 0, t:t + 1]
             src = gb[g][:, t, :].bitcast(FP8)
             if on_vector:
                 nc.vector.tensor_scalar(out=gw[g][:, t, :], in0=src, scalar1=sc, scalar2=None, op0=MULT)
@@ -112,32 +111,6 @@ def tile_meg_forward_whitened_d3_kernel(tc, g_bytes, g_scale, j_in, gain_in, e_i
                 nc.scalar.copy(out=dst, in_=src)
             else:
                 nc.vector.tensor_copy(out=dst, in_=src)
-
-        def j_interleave_pe(c, g):
-            ji[c, g] = work.tile([P, W, 4], BF16, name="ji", bufs=6, align_bytes=64)
-            flat = ji[c, g][:].rearrange("p n t -> p (n t)")
-            for q in range(2):
-                xp = psum.tile([P, 1024], BF16, name="bank%d" % (4 + turn[0] % 4))
-                turn[0] += 1
-                for h in range(2):
-                    n0 = 256 * q + 128 * h
-                    if CFG["form"] == 0:
-                        nc.tensor.matmul(
-                            out=xp[:, 512 * h:512 * (h + 1)].rearrange("p (n t) -> p t n", t=4),
-                            lhsT=ident_b[:],
-                            rhs=jr[c, g][:, :, n0:n0 + 128],
-                            start=True,
-                            stop=True,
-                        )
-                    else:
-                        nc.tensor.matmul(
-                            out=xp[:, 512 * h:512 * (h + 1)].rearrange("p (n t) -> p n t", t=4),
-                            lhsT=ident_b[:],
-                            rhs=jr[c, g][:, :, n0:n0 + 128].rearrange("p t n -> p n t"),
-                            start=True,
-                            stop=True,
-                        )
-                nc.scalar.copy(out=flat[:, 1024 * q:1024 * (q + 1)], in_=xp[:])
 
         def j_quant(c, g):
             jc[c, g] = keep.tile([P, W], U32, name="jc%d_%d" % (c, g), align_bytes=64)
@@ -266,7 +239,7 @@ def tile_meg_forward_whitened_d3_kernel(tc, g_bytes, g_scale, j_in, gain_in, e_i
             for g in range(PASSES):
                 on_scalar = g in CFG["sj"][0]
                 on_scalar = on_scalar or g in CFG["pj"][0]
-                do_s = j_interleave_pe if g in CFG["pj"][0] else (lambda c, g: j_interleave(c, g, True))
+                do_s = lambda c, g: j_interleave(c, g, True)
                 if on_scalar and CFG["jfirst"]:
                     do_s(0, g)
                 if g + 1 < PASSES:
@@ -288,10 +261,7 @@ def tile_meg_forward_whitened_d3_kernel(tc, g_bytes, g_scale, j_in, gain_in, e_i
             for g in range(PASSES):
                 on_scalar = g in CFG["sj"][1]
                 on_scalar = on_scalar or g in CFG["pj"][1]
-                if g in CFG["pj"][1]:
-                    j_interleave_pe(1, g)
-                else:
-                    j_interleave(1, g, on_scalar)
+                j_interleave(1, g, on_scalar)
                 flush(0 if g == 0 else CFG["lag"])
                 if g == CFG["vq"]:
                     v_quant()

@@ -21,7 +21,7 @@ PASSES = SRC // 512
 NCH = 2
 W = TIM // NCH
 
-CFG = {'sj': ((3, 4, 7), (0, 2, 4, 5, 6)), 'vw': (3, 0, 0, 0, 0, 1, 0, 0), 'jfirst': 0, 'st': (1, 1, 3, 4), 'bi': (7, 1), 'bq': 7, 'ev': 7, 'vc': 5, 'vq': 7, 'tail': (0, 0), 'evv': (2, 3, 4, 5), 'lag': 0, 'pj': ((), ()), 'late': 0, 'gfirst': 1, 'form': 0}
+CFG = {'sj': ((1, 3, 4, 7), (0, 2, 4, 5, 6)), 'vw': (2, 0, 0, 1, 1, 2, 1, 0), 'jfirst': 0, 'st': (1, 4, 4, 5), 'bi': (7, 1), 'bq': 7, 'ev': 8, 'vc': 5, 'vq': 7, 'tail': (0, 0), 'evv': (2, 3, 7), 'lag': 0, 'pj': ((3, 5, 7), ()), 'late': 0, 'gfirst': 1, 'form': 0}
 
 
 def tile_meg_forward_whitened_d3_kernel(tc, g_bytes, g_scale, j_in, gain_in, e_in, v_in, out):
@@ -36,6 +36,9 @@ def tile_meg_forward_whitened_d3_kernel(tc, g_bytes, g_scale, j_in, gain_in, e_i
         make_identity(nc, ident_raw[:])
         ident = keep.tile([P, P], F32, name="ident")
         nc.scalar.activation(out=ident[:], in_=ident_raw[:], func=COPY)
+
+        ident_b = keep.tile([P, P], BF16, name="ident_b")
+        nc.vector.tensor_copy(out=ident_b[:], in_=ident_raw[:])
 
         gsc = {}
         gs_view = g_scale.rearrange("(g p t) o -> p g (t o)", p=P, t=4)
@@ -112,6 +115,31 @@ def tile_meg_forward_whitened_d3_kernel(tc, g_bytes, g_scale, j_in, gain_in, e_i
             else:
                 nc.vector.tensor_copy(out=dst, in_=src)
 
+        packed = {}
+
+        def next_bank():
+            turn[0] += 1
+            return "bank%d" % (4 + (turn[0] - 1) % 4)
+
+        def pe_pack(g):
+            for q in range(2):
+                packed[g, q] = psum.tile([P, 1024], BF16, name=next_bank())
+                for h in range(2):
+                    n0 = 256 * q + 128 * h
+                    nc.tensor.matmul(
+                        out=packed[g, q][:, 512 * h:512 * (h + 1)].rearrange("p (n t) -> p t n", t=4),
+                        lhsT=ident_b[:],
+                        rhs=jr[0, g][:, :, n0:n0 + 128],
+                        start=True,
+                        stop=True,
+                    )
+
+        def pe_fetch(g):
+            ji[0, g] = work.tile([P, W, 4], BF16, name="ji", bufs=6, align_bytes=64)
+            flat = ji[0, g][:].rearrange("p n t -> p (n t)")
+            for q in range(2):
+                nc.scalar.copy(out=flat[:, 1024 * q:1024 * (q + 1)], in_=packed[g, q][:])
+
         def j_quant(c, g):
             jc[c, g] = keep.tile([P, W], U32, name="jc%d_%d" % (c, g), align_bytes=64)
             js[c, g] = keep.tile([P, W], U8, name="js%d_%d" % (c, g), align_bytes=64)
@@ -141,7 +169,7 @@ def tile_meg_forward_whitened_d3_kernel(tc, g_bytes, g_scale, j_in, gain_in, e_i
         def v_transpose():
             words = v_raw[:].rearrange("p b s -> p (b s)").bitcast(F32)
             for h in range(2):
-                vt[h] = psum.tile([P, 2, 2, P], F32, name="bank%d" % (4 + h))
+                vt[h] = psum.tile([P, 2, 2, P], F32, name=next_bank())
                 for b in range(2):
                     for u in range(2):
                         w0 = (2 * h + b) * 256
@@ -239,13 +267,17 @@ def tile_meg_forward_whitened_d3_kernel(tc, g_bytes, g_scale, j_in, gain_in, e_i
             for g in range(PASSES):
                 on_scalar = g in CFG["sj"][0]
                 on_scalar = on_scalar or g in CFG["pj"][0]
-                do_s = lambda c, g: j_interleave(c, g, True)
+                do_s = lambda c, g: pe_fetch(g) if g in CFG["pj"][0] else j_interleave(c, g, True)
+                if g == 0 and 0 in CFG["pj"][0]:
+                    pe_pack(0)
                 if on_scalar and CFG["jfirst"]:
                     do_s(0, g)
                 if g + 1 < PASSES:
                     widen_all(g + 1)
                 if on_scalar and not CFG["jfirst"]:
                     do_s(0, g)
+                if g + 1 in CFG["pj"][0]:
+                    pe_pack(g + 1)
                 if g == CFG["vc"]:
                     v_transpose()
                     v_copy(0)
@@ -288,6 +320,12 @@ def tile_meg_forward_whitened_d3_kernel(tc, g_bytes, g_scale, j_in, gain_in, e_i
             for h in range(2):
                 for m in range(4):
                     gain_noise(1, m, h, 2)
+                if h == 0 and CFG["bq"] == 8:
+                    b_quant(0, 0, 1)
+                    stage2(0, 0, 1)
+                if h == 0 and CFG["ev"] == 8:
+                    for b in range(4):
+                        finish(0, 0, b, 1, True)
                 if h == 1:
                     b_quant(1, 0, 2)
                     stage2(1, 0, 2)

from contextlib import ExitStack

import concourse.mybir as mybir
from concourse.masks import make_identity

SRC, SEN, TIM = 4096, 512, 1024
FLOPS = 2 * SRC * SEN * TIM + 2 * SEN * SEN * TIM

F32 = mybir.dt.float32
BF16 = mybir.dt.bfloat16
U32 = mybir.dt.uint32
U8 = mybir.dt.uint8
FP8 = mybir.dt.float8_e4m3fn
FP8X4 = mybir.dt.float8_e4m3fn_x4
MULT = mybir.AluOpType.mult
ADD = mybir.AluOpType.add
COPY = mybir.ActivationFunctionType.Copy

P = 128
PASSES = SRC // 512
NCH = 2
W = TIM // NCH

CFG = {'sj': ((1, 3, 4, 7), (0, 2, 4, 5, 6)), 'vw': (2, 0, 0, 1, 1, 2, 1, 0), 'jfirst': 0, 'st': (1, 4, 4, 5), 'bi': (7, 1), 'bq': 7, 'ev': 8, 'vc': 5, 'vq': 7, 'tail': (0, 0), 'evv': (2, 3, 7), 'lag': 0, 'pj': ((3, 5, 7), ()), 'late': 0, 'gfirst': 1, 'form': 0}


def tile_meg_forward_whitened_d3_kernel(tc, g_bytes, g_scale, j_in, gain_in, e_in, v_in, out):
    nc = tc.nc

    with ExitStack() as ctx:
        keep = ctx.enter_context(tc.tile_pool(name="keep", bufs=1))
        work = ctx.enter_context(tc.tile_pool(name="work", bufs=3))
        psum = ctx.enter_context(tc.psum_pool(name="psum", bufs=1))

        ident_raw = keep.tile([P, P], F32, name="ident_raw")
        make_identity(nc, ident_raw[:])
        ident = keep.tile([P, P], F32, name="ident")
        nc.scalar.activation(out=ident[:], in_=ident_raw[:], func=COPY)

        ident_b = keep.tile([P, P], BF16, name="ident_b")
        nc.vector.tensor_copy(out=ident_b[:], in_=ident_raw[:])

        gsc = {}
        gs_view = g_scale.rearrange("(g p t) o -> p g (t o)", p=P, t=4)
        gb_view = g_bytes.rearrange("(g p t) s -> g p t s", p=P, t=4)
        j_view = j_in.rearrange("(g p t) n -> g p t n", p=P, t=4)
        gb, jr = {}, {}

        def load_g(g):
            gb[g] = keep.tile([P, 4, SEN], U8, name="gb%d" % g, align_bytes=64)
            gsc[g] = keep.tile([P, 1, 4], F32, name="gsc%d" % g)
            nc.sync.dma_start(out=gsc[g][:], in_=gs_view[:, g:g + 1, :])
            for t in range(0, 4, 2) if g == 0 else ():
                nc.sync.dma_start(out=gb[g][:, t:t + 2, :], in_=gb_view[g][:, t:t + 2, :])
            if g > 0:
                nc.sync.dma_start(out=gb[g][:], in_=gb_view[g])

        def load_j(c, g):
            jr[c, g] = work.tile([P, 4, W], BF16, name="jr", bufs=12, align_bytes=64)
            nc.sync.dma_start(out=jr[c, g][:], in_=j_view[g][:, :, c * W:(c + 1) * W])

        v_raw = keep.tile([P, 4, SEN], BF16, name="v_raw", align_bytes=64)
        for g in range(CFG["gfirst"]):
            load_g(g)
        for g in range(PASSES):
            if g + CFG["gfirst"] < PASSES:
                load_g(g + CFG["gfirst"])
            load_j(0, g)
            if g == 3:
                nc.sync.dma_start(out=v_raw[:], in_=v_in.rearrange("(b p) s -> p b s", p=P))
        gain = keep.tile([P, 4], BF16, name="gain")
        nc.sync.dma_start(out=gain[:], in_=gain_in.rearrange("(p t) -> p t", t=4))
        for g in range(PASSES):
            load_j(1, g)
            if g == 3:
                e_sb = keep.tile([P, 4, TIM], BF16, name="e_sb", align_bytes=64)
                nc.sync.dma_start(out=e_sb[:], in_=e_in.rearrange("(p t) n -> p t n", t=4))

        gw, gi, ji = {}, {}, {}
        gc, gs, jc, js = {}, {}, {}, {}
        acc = {}
        bank_of = {0: 0, 1: 0 if CFG["late"] else 4}
        turn = [0]

        def widen(g, t, on_vector=False):
            if t == 0:
                gw[g] = work.tile([P, 4, SEN], BF16, name="gw", align_bytes=64)
            sc = gsc[g][:, 0, t:t + 1]
            src = gb[g][:, t, :].bitcast(FP8)
            if on_vector:
                nc.vector.tensor_scalar(out=gw[g][:, t, :], in0=src, scalar1=sc, scalar2=None, op0=MULT)
            else:
                nc.scalar.activation(out=gw[g][:, t, :], in_=src, func=COPY, scale=sc)

        def g_interleave(g):
            gi[g] = work.tile([P, SEN, 4], BF16, name="gi", align_bytes=64)
            nc.vector.tensor_copy(
                out=gi[g][:].rearrange("p (t m) j -> p m j t", t=4),
                in_=gw[g][:].rearrange("p j (m t) -> p m j t", t=4),
            )

        def g_quant(g):
            gc[g] = keep.tile([P, SEN], U32, name="gc%d" % g, align_bytes=64)
            gs[g] = keep.tile([P, SEN], U8, name="gs%d" % g, align_bytes=64)
            nc.vector.quantize_mx(
                out=gc[g][:].bitcast(FP8X4), scales=gs[g][:], in_=gi[g][:].rearrange("p n t -> p (n t)")
            )

        def j_interleave(c, g, on_scalar):
            ji[c, g] = work.tile([P, W, 4], BF16, name="ji", bufs=6, align_bytes=64)
            dst = ji[c, g][:].rearrange("p (c i) t -> p c t i", i=4)
            src = jr[c, g][:].rearrange("p t (c i) -> p c t i", i=4)
            if on_scalar:
                nc.scalar.copy(out=dst, in_=src)
            else:
                nc.vector.tensor_copy(out=dst, in_=src)

        packed = {}

        def next_bank():
            turn[0] += 1
            return "bank%d" % (4 + (turn[0] - 1) % 4)

        def pe_pack(g):
            for q in range(2):
                packed[g, q] = psum.tile([P, 1024], BF16, name=next_bank())
                for h in range(2):
                    n0 = 256 * q + 128 * h
                    nc.tensor.matmul(
                        out=packed[g, q][:, 512 * h:512 * (h + 1)].rearrange("p (n t) -> p t n", t=4),
                        lhsT=ident_b[:],
                        rhs=jr[0, g][:, :, n0:n0 + 128],
                        start=True,
                        stop=True,
                    )

        def pe_fetch(g):
            ji[0, g] = work.tile([P, W, 4], BF16, name="ji", bufs=6, align_bytes=64)
            flat = ji[0, g][:].rearrange("p n t -> p (n t)")
            for q in range(2):
                nc.scalar.copy(out=flat[:, 1024 * q:1024 * (q + 1)], in_=packed[g, q][:])

        def j_quant(c, g):
            jc[c, g] = keep.tile([P, W], U32, name="jc%d_%d" % (c, g), align_bytes=64)
            js[c, g] = keep.tile([P, W], U8, name="js%d_%d" % (c, g), align_bytes=64)
            nc.vector.quantize_mx(
                out=jc[c, g][:].bitcast(FP8X4), scales=js[c, g][:], in_=ji[c, g][:].rearrange("p n t -> p (n t)")
            )

        def stage1(c, g):
            for m in range(4):
                if g == 0:
                    acc[c, m] = psum.tile([P, W], F32, name="bank%d" % (bank_of[c] + m))
                nc.tensor.matmul_mx(
                    out=acc[c, m][:],
                    lhsT=gc[g][:, m * P:(m + 1) * P].bitcast(FP8X4),
                    lhsT_scale=gs[g][:, m * P:(m + 1) * P],
                    rhs=jc[c, g][:].bitcast(FP8X4),
                    rhs_scale=js[c, g][:],
                    start=(g == 0),
                    stop=(g == PASSES - 1),
                )

        v_grp = keep.tile([P, SEN, 4], BF16, name="v_grp", align_bytes=64)
        v_codes = keep.tile([P, SEN], U32, name="v_codes", align_bytes=64)
        v_scales = keep.tile([P, SEN], U8, name="v_scales", align_bytes=64)
        vt = {}

        def v_transpose():
            words = v_raw[:].rearrange("p b s -> p (b s)").bitcast(F32)
            for h in range(2):
                vt[h] = psum.tile([P, 2, 2, P], F32, name=next_bank())
                for b in range(2):
                    for u in range(2):
                        w0 = (2 * h + b) * 256
                        nc.tensor.transpose(vt[h][:, b, u, :], words[:, w0 + u:w0 + 256:2], ident[:])

        def v_copy(h):
            dst = v_grp[:].rearrange("p w t -> p (w t)").bitcast(F32)[:, 512 * h:512 * (h + 1)]
            nc.scalar.copy(
                out=dst.rearrange("p (b r u) -> p b r u", b=2, u=2), in_=vt[h][:].rearrange("p b u r -> p b r u")
            )

        def v_quant():
            nc.vector.quantize_mx(
                out=v_codes[:].bitcast(FP8X4), scales=v_scales[:], in_=v_grp[:].rearrange("p w t -> p (w t)")
            )

        bp, bi, bc, bs, y, acc2 = {}, {}, {}, {}, {}, {}

        def gain_noise(c, m, h, parts):
            n = W // parts
            if m == 0:
                bp[c, h] = work.tile([P, 4, n], BF16, name="bp%d" % n, bufs=parts, align_bytes=64)
            nc.vector.scalar_tensor_tensor(
                out=bp[c, h][:, m, :],
                in0=acc[c, m][:, h * n:(h + 1) * n],
                scalar=gain[:, m:m + 1],
                in1=e_sb[:, m, c * W + h * n:c * W + (h + 1) * n],
                op0=MULT,
                op1=ADD,
            )

        def b_interleave(c, h, parts, on_scalar):
            n = W // parts
            bi[c, h] = work.tile([P, n, 4], BF16, name="bi%d" % n, bufs=parts, align_bytes=64)
            dst = bi[c, h][:].rearrange("p (c i) t -> p c t i", i=4)
            src = bp[c, h][:].rearrange("p t (c i) -> p c t i", i=4)
            if on_scalar:
                nc.scalar.copy(out=dst, in_=src)
            else:
                nc.vector.tensor_copy(out=dst, in_=src)

        def b_quant(c, h, parts):
            n = W // parts
            bc[c, h] = work.tile([P, n], U32, name="bc%d" % n, bufs=parts, align_bytes=64)
            bs[c, h] = work.tile([P, n], U8, name="bs%d" % n, bufs=parts, align_bytes=64)
            nc.vector.quantize_mx(
                out=bc[c, h][:].bitcast(FP8X4), scales=bs[c, h][:], in_=bi[c, h][:].rearrange("p n t -> p (n t)")
            )

        def stage2(c, h, parts):
            n = W // parts
            for b in range(4):
                bank = ((4 if CFG["late"] else 0) if c == 0 else 4 * h) + b
                if c == 1 and CFG["late"]:
                    bank = 4 * (1 - h) + b
                acc2[c, h, b] = psum.tile([P, n], F32, name="bank%d" % bank)
                nc.tensor.matmul_mx(
                    out=acc2[c, h, b][:],
                    lhsT=v_codes[:, b * P:(b + 1) * P].bitcast(FP8X4),
                    lhsT_scale=v_scales[:, b * P:(b + 1) * P],
                    rhs=bc[c, h][:].bitcast(FP8X4),
                    rhs_scale=bs[c, h][:],
                    start=True,
                    stop=True,
                )

        def finish(c, h, b, parts, on_scalar):
            n = W // parts
            y = work.tile([P, n], F32, name="y%d" % n, bufs=4 * parts)
            if on_scalar:
                nc.scalar.copy(out=y[:], in_=acc2[c, h, b][:])
            else:
                nc.vector.tensor_copy(out=y[:], in_=acc2[c, h, b][:])
            nc.sync.dma_start(out=out[b * P:(b + 1) * P, c * W + h * n:c * W + (h + 1) * n], in_=y[:])

        with tc.manual_schedule():
            pending = []

            held = []

            def flush(keep_back):
                while len(pending) > keep_back:
                    c, g = pending.pop(0)
                    j_quant(c, g)
                    if CFG["late"] and c == 1 and not bp.get("done"):
                        held.append(g)
                    else:
                        stage1(c, g)

            def widen_all(g):
                for t in range(4):
                    widen(g, t, on_vector=t >= 4 - CFG["vw"][g])

            widen_all(0)
            for g in range(PASSES):
                on_scalar = g in CFG["sj"][0]
                on_scalar = on_scalar or g in CFG["pj"][0]
                do_s = lambda c, g: pe_fetch(g) if g in CFG["pj"][0] else j_interleave(c, g, True)
                if g == 0 and 0 in CFG["pj"][0]:
                    pe_pack(0)
                if on_scalar and CFG["jfirst"]:
                    do_s(0, g)
                if g + 1 < PASSES:
                    widen_all(g + 1)
                if on_scalar and not CFG["jfirst"]:
                    do_s(0, g)
                if g + 1 in CFG["pj"][0]:
                    pe_pack(g + 1)
                if g == CFG["vc"]:
                    v_transpose()
                    v_copy(0)
                    v_copy(1)
                g_interleave(g)
                if not on_scalar:
                    j_interleave(0, g, False)
                flush(CFG["lag"])
                g_quant(g)
                pending.append((0, g))
                if not on_scalar:
                    flush(CFG["lag"])
            for g in range(PASSES):
                on_scalar = g in CFG["sj"][1]
                on_scalar = on_scalar or g in CFG["pj"][1]
                j_interleave(1, g, on_scalar)
                flush(0 if g == 0 else CFG["lag"])
                if g == CFG["vq"]:
                    v_quant()
                for m in range(4):
                    if CFG["st"][m] == g:
                        gain_noise(0, m, 0, 1)
                        if m == 3:
                            bp["done"] = True
                            for k in held:
                                stage1(1, k)
                            held.clear()
                pending.append((1, g))
                if not on_scalar:
                    flush(CFG["lag"])
                if g == CFG["bi"][0]:
                    b_interleave(0, 0, 1, CFG["bi"][1])
                if g == CFG["bq"]:
                    b_quant(0, 0, 1)
                    stage2(0, 0, 1)
                if g == CFG["ev"]:
                    for b in range(4):
                        finish(0, 0, b, 1, True)
            flush(0)
            for h in range(2):
                for m in range(4):
                    gain_noise(1, m, h, 2)
                if h == 0 and CFG["bq"] == 8:
                    b_quant(0, 0, 1)
                    stage2(0, 0, 1)
                if h == 0 and CFG["ev"] == 8:
                    for b in range(4):
                        finish(0, 0, b, 1, True)
                if h == 1:
                    b_quant(1, 0, 2)
                    stage2(1, 0, 2)
                b_interleave(1, h, 2, CFG["tail"][h])
            b_quant(1, 1, 2)
            stage2(1, 1, 2)
            for h in range(2):
                for b in range(4):
                    finish(1, h, b, 2, (4 * h + b) not in CFG["evv"])
